import numpy as np
import ml_dtypes


def mxq(x, axis, fmt="e4m3"):
    dtype, down = {"e4m3": (ml_dtypes.float8_e4m3fn, 7), "e5m2": (ml_dtypes.float8_e5m2, 14)}[fmt]
    v = np.moveaxis(np.asarray(x, np.float32).astype(ml_dtypes.bfloat16).astype(np.float64), axis, -1)
    blocks = v.reshape(v.shape[:-1] + (-1, 32))
    amax = np.abs(blocks).max(-1, keepdims=True)
    byte = np.maximum(np.where(amax > 0, np.frexp(amax)[1] - 1 + 127, 0) - down, 1)
    scale = np.exp2(byte - 127.0)
    codes = (blocks / scale).astype(np.float32).astype(dtype).astype(np.float64)
    return np.moveaxis((codes * scale).reshape(v.shape), -1, axis)


WIDE = False


def mx_kscale(k, group=512):
    if not WIDE:
        return np.ones(k)
    levels = np.array([10, -10, 5, -5, 0])
    if group != 512:
        return np.exp2(np.random.permutation(np.resize(levels, k // group))).repeat(group)
    if k % 512:
        return np.exp2(np.random.permutation(np.resize(levels, k // 32))).repeat(32)
    a = np.empty((k // 512, 16))
    for p in range(k // 512):
        a[p, :8] = np.random.permutation(np.resize(levels, 8))
        for g in range(8):
            far = levels[np.abs(levels - a[p, g]) >= 10]
            a[p, g + 8] = far[np.random.randint(len(far))]
    return np.exp2(a.ravel()).repeat(32)


def f64(x):
    return np.asarray(x).astype(np.float64)


def sigmoid(v):
    return 1.0 / (1.0 + np.exp(-v))


def bf(x):
    return np.asarray(x, np.float32).astype(ml_dtypes.bfloat16)


def planes(Y):
    r, m = Y.shape
    b = f64(bf(Y)).reshape(r // 32, 32, m)
    amax = np.abs(b).max(1)
    byte = np.clip(np.where(amax > 0, np.frexp(amax)[1] - 1 + 127 - 7, 1), 1, 254)
    codes = (b * np.exp2(127.0 - byte)[:, None, :]).reshape(r, m).astype(np.float32).astype(ml_dtypes.float8_e4m3fn).view(np.uint8)
    words = codes.reshape(r // 512, 128, 4, m).transpose(0, 1, 3, 2)
    return np.ascontiguousarray(words), np.ascontiguousarray(byte.astype(np.uint8).reshape(r // 512, 16, m))


G, D, M, N = 2, 256, 256, 512


def setup_inputs():
    n = np.random.standard_normal
    s_d = mx_kscale(D, 0)
    return {
        "h": (n((G, D, N)) * s_d[:, None]).astype(np.float32),
        "wt": (n((G, D, M)) / np.sqrt(D) / s_d[:, None]).astype(np.float32),
        "wc": (n((G, D, M)) / np.sqrt(D) / s_d[:, None]).astype(np.float32),
        "xr": (n((G, M, N))).astype(np.float32),
        "bt": (0.5 * n((G, M, 1))).astype(np.float32),
        "bc": (0.5 * n((G, M, 1))).astype(np.float32),
    }


def reference(h, wt, wc, xr, bt, bc):
    wtq = mxq(f64(wt), 1, "e4m3")
    hq = mxq(f64(h), 1, "e4m3")
    zt = wtq.transpose(0, 2, 1) @ hq
    wcq = mxq(f64(wc), 1, "e4m3")
    zc = wcq.transpose(0, 2, 1) @ hq
    t = sigmoid(zt + f64(bt))
    y = t * np.maximum(zc + f64(bc), 0.0) + (1.0 - t) * f64(xr)
    Y = y.reshape(G * M, N)
    words, scales = planes(Y)
    return Y, words, scales

@@ -1,0 +1,180 @@
+from contextlib import ExitStack
+
+import concourse.mybir as mybir
+
+G, D, M, N = 2, 256, 256, 512
+FLOPS = 2 * 2 * G * D * M * N
+
+F32 = mybir.dt.float32
+BF16 = mybir.dt.bfloat16
+U32 = mybir.dt.uint32
+I32 = mybir.dt.int32
+U8 = mybir.dt.uint8
+FP8X4 = mybir.dt.float8_e4m3fn_x4
+ACT = mybir.ActivationFunctionType
+ALU = mybir.AluOpType
+
+P = 128
+R = 64
+PACK = 4
+HALF = N // 2
+H_SPLIT = 352
+W_SPLIT = 40
+
+
+def tile_rows_pl_cell_hwy_kernel(tc, h, wt, wc, xr, bt, bc, out_0, out_1, out_2):
+    nc = tc.nc
+    with ExitStack() as ctx:
+        sb = ctx.enter_context(tc.tile_pool(name="sb", bufs=1))
+        ps = ctx.enter_context(tc.psum_pool(name="ps", bufs=2))
+        ctx.enter_context(tc.manual_schedule())
+
+        h_rows = h.rearrange("g (s j) n -> (g s) j n", j=PACK)
+        x_rows = xr.rearrange("g (s u) n -> (g s) u n", u=PACK)
+        y_rows = out_0.rearrange("(p u) n -> p u n", u=PACK)
+
+        h_raw = [sb.tile([P, 2, N], F32, name="h_raw%d" % i) for i in range(2)]
+        w_raw = {k: sb.tile([P, PACK, M], F32, name="w_raw_" + k) for k in "tc"}
+        x = [sb.tile([P, N], F32, name="x%d" % u) for u in range(PACK)]
+        bias = {k: sb.tile([P, PACK], F32, name="bias_" + k) for k in "tc"}
+
+        for i in range(2):
+            nc.sync.dma_start(out=h_raw[i][:], in_=h_rows[:, 2 * i : 2 * i + 2, :])
+        for k, w, b in (("t", wt, bt), ("c", wc, bc)):
+            nc.sync.dma_start(out=w_raw[k][:], in_=w.rearrange("g (s j) m -> (g s) j m", j=PACK))
+            nc.scalar.dma_start(out=bias[k][:], in_=b.rearrange("g (s u) o -> (g s) (u o)", u=PACK))
+        for u in range(PACK):
+            nc.sync.dma_start(out=x[u][:], in_=x_rows[:, u, :])
+
+        w_codes = {k: sb.tile([P, 6 * R], U32, name="w_codes_" + k, align_bytes=64) for k in "tc"}
+        w_scales = {k: sb.tile([P, 6 * R], U8, name="w_scales_" + k, align_bytes=64) for k in "tc"}
+        warm = sb.tile([P, 8], F32, name="warm")
+        warm_out = sb.tile([P, 8], F32, name="warm_out")
+        nc.vector.memset(warm[:], 0.0)
+        nc.scalar.activation(out=warm_out[:], in_=warm[:], func=ACT.Sigmoid)
+        for k in "tc":
+            nc.vector.memset(w_codes[k][:], 0)
+            nc.vector.memset(w_scales[k][:].bitcast(U32), 0)
+
+        h_bf = sb.tile([P, N, PACK], BF16, name="h_bf", align_bytes=64)
+        h_codes = sb.tile([P, N], U32, name="h_codes", align_bytes=64)
+        h_scales = sb.tile([P, N], U8, name="h_scales", align_bytes=64)
+        nc.vector.tensor_copy(out=h_bf[:, :, 0:2], in_=h_raw[0][:].rearrange("p j n -> p n j"))
+        nc.vector.tensor_copy(out=h_bf[:, :H_SPLIT, 2:4], in_=h_raw[1][:, :, :H_SPLIT].rearrange("p j n -> p n j"))
+        nc.scalar.copy(out=h_bf[:, H_SPLIT:, 2:4], in_=h_raw[1][:, :, H_SPLIT:].rearrange("p j n -> p n j"))
+        nc.vector.quantize_mx(out=h_codes[:].bitcast(FP8X4), scales=h_scales[:], in_=h_bf[:].rearrange("p n j -> p (n j)"))
+
+        def quantise_weights(k):
+            w_bf = sb.tile([P, PACK, R, PACK], BF16, name="w_bf_" + k, align_bytes=64)
+            dst = w_bf[:].rearrange("p u s j -> p s j u")
+            src = w_raw[k][:].rearrange("p j (s u) -> p s j u", u=PACK)
+            nc.vector.tensor_copy(out=dst[:, :W_SPLIT], in_=src[:, :W_SPLIT])
+            nc.scalar.copy(out=dst[:, W_SPLIT:], in_=src[:, W_SPLIT:])
+            nc.vector.quantize_mx(
+                out=w_codes[k][:, R : 5 * R].bitcast(FP8X4),
+                scales=w_scales[k][:, R : 5 * R],
+                in_=w_bf[:].rearrange("p u s j -> p (u s j)"),
+            )
+
+        z = {}
+
+        def product(k, u):
+            for g in range(G):
+                rows = slice(R * g, R * g + R)
+                cols = slice(R * (u + 1 - g), R * (u + 3 - g))
+                z[k, u, g] = ps.tile([P, N], F32, name="z_%s%d" % (k, g))
+                nc.tensor.matmul_mx(
+                    out=z[k, u, g][:],
+                    lhsT=w_codes[k][rows, cols].bitcast(FP8X4),
+                    lhsT_scale=w_scales[k][rows, cols],
+                    rhs=h_codes[rows, :].bitcast(FP8X4),
+                    rhs_scale=h_scales[rows, :],
+                    start=True,
+                    stop=True,
+                )
+
+        t = [sb.tile([P, N], F32, name="t%d" % u) for u in range(PACK)]
+        r = [sb.tile([P, N], F32, name="r%d" % u) for u in range(2)]
+        a = [sb.tile([P, N], F32, name="a%d" % u) for u in range(PACK)]
+        b = [sb.tile([P, N], F32, name="b%d" % u) for u in range(PACK)]
+        y_lo = sb.tile([P, 2, N], F32, name="y_lo")
+        y_hi = [sb.tile([P, 2, HALF], F32, name="y_hi%d" % i) for i in range(2)]
+        y_bf = [sb.tile([P, HALF, PACK], BF16, name="y_bf%d" % i, align_bytes=64) for i in range(2)]
+        y_codes = sb.tile([P, N], U32, name="y_codes", align_bytes=64)
+        y_scales = sb.tile([P, N], U8, name="y_scales", align_bytes=64)
+
+        def from_psum(func, k, u, dst):
+            for g in range(G):
+                rows = slice(R * g, R * g + R)
+                nc.scalar.activation(out=dst[rows, :], in_=z[k, u, g][rows, :], func=func, bias=bias[k][rows, u : u + 1])
+
+        def gated_from_psum(u):
+            for g in range(G):
+                rows = slice(R * g, R * g + R)
+                nc.vector.scalar_tensor_tensor(
+                    out=a[u][rows, :], in0=z["c", u, g][rows, :], scalar=bias["c"][rows, u : u + 1], in1=t[u][rows, :],
+                    op0=ALU.add, op1=ALU.mult,
+                )
+
+        def carried(u, cols):
+            nc.vector.scalar_tensor_tensor(
+                out=b[u][:, cols], in0=t[u][:, cols], scalar=1.0, in1=x[u][:, cols], op0=ALU.subtract, op1=ALU.mult
+            )
+
+        def gated(u, cols):
+            nc.vector.tensor_tensor(out=a[u][:, cols], in0=r[u - 2][:, cols], in1=t[u][:, cols], op=ALU.mult)
+
+        def combine(u, cols, dst):
+            nc.vector.scalar_tensor_tensor(
+                out=dst, in0=a[u][:, cols], scalar=0.0, in1=b[u][:, cols], op0=ALU.max, op1=ALU.subtract
+            )
+
+        whole = slice(0, N)
+        halves = [slice(0, HALF), slice(HALF, N)]
+
+        quantise_weights("t")
+        product("t", 0)
+        product("t", 1)
+        quantise_weights("c")
+        from_psum(ACT.Sigmoid, "t", 0, t[0])
+        product("c", 0)
+        product("c", 1)
+        from_psum(ACT.Sigmoid, "t", 1, t[1])
+        product("t", 2)
+        product("t", 3)
+        from_psum(ACT.Sigmoid, "t", 2, t[2])
+        from_psum(ACT.Sigmoid, "t", 3, t[3])
+        for u in range(2):
+            gated_from_psum(u)
+            carried(u, whole)
+            product("c", u + 2)
+            if u == 1:
+                combine(0, whole, y_lo[:, 0, :])
+                nc.sync.dma_start(out=y_rows[:, 0, :], in_=y_lo[:, 0, :])
+        carried(2, whole)
+        combine(1, whole, y_lo[:, 1, :])
+        nc.sync.dma_start(out=y_rows[:, 1, :], in_=y_lo[:, 1, :])
+        from_psum(ACT.Relu, "c", 2, r[0])
+        from_psum(ACT.Relu, "c", 3, r[1])
+        carried(3, whole)
+        for i in range(2):
+            nc.scalar.copy(out=y_bf[i][:, :, 0:2], in_=y_lo[:, :, halves[i]].rearrange("p u n -> p n u"))
+        for i in range(2):
+            gated(2, halves[i])
+            gated(3, halves[i])
+            combine(2, halves[i], y_hi[i][:, 0, :])
+            combine(3, halves[i], y_hi[i][:, 1, :])
+            nc.sync.dma_start(out=y_rows[:, 2:4, halves[i]], in_=y_hi[i][:])
+            cast = nc.scalar.copy if i == 0 else nc.vector.tensor_copy
+            cast(out=y_bf[i][:, :, 2:4], in_=y_hi[i][:].rearrange("p u n -> p n u"))
+        words = out_1.rearrange("o p n u -> (o p) (n u)").bitcast(I32)
+        for i in range(2):
+            nc.vector.quantize_mx(
+                out=y_codes[:, halves[i]].bitcast(FP8X4), scales=y_scales[:, halves[i]],
+                in_=y_bf[i][:].rearrange("p n u -> p (n u)"),
+            )
+            nc.sync.dma_start(out=words[:, halves[i]], in_=y_codes[:, halves[i]].bitcast(I32))
+        scale_rows = out_2.rearrange("o f n -> (o f) n").bitcast(I32)
+        for q in range(4):
+            queue = nc.scalar if q % 2 else nc.sync
+            queue.dma_start(out=scale_rows[4 * q : 4 * q + 4, :], in_=y_scales[32 * q : 32 * q + 4, :].bitcast(I32))

@@ -19,7 +19,7 @@ R = 64
 PACK = 4
 HALF = N // 2
 H_SPLIT = 352
-W_SPLIT = 40
+LOW, HIGH = 0, 1
 
 
 def tile_rows_pl_cell_hwy_kernel(tc, h, wt, wc, xr, bt, bc, out_0, out_1, out_2):
@@ -29,148 +29,195 @@ def tile_rows_pl_cell_hwy_kernel(tc, h, wt, wc, xr, bt, bc, out_0, out_1, out_2)
         ps = ctx.enter_context(tc.psum_pool(name="ps", bufs=2))
         ctx.enter_context(tc.manual_schedule())
 
-        h_rows = h.rearrange("g (s j) n -> (g s) j n", j=PACK)
-        x_rows = xr.rearrange("g (s u) n -> (g s) u n", u=PACK)
-        y_rows = out_0.rearrange("(p u) n -> p u n", u=PACK)
+        whole = slice(0, N)
+        halves = [slice(0, HALF), slice(HALF, N)]
+        rows_of = [slice(R * g, R * (g + 1)) for g in range(G)]
 
+        units = [(LOW, 0), (LOW, 1), (HIGH, 2), (HIGH, 3)]
+
+        def unit_tiles(name, which):
+            return {unit: sb.tile([P, N], F32, name="%s%d" % (name, unit[1])) for unit in which}
+
+        h_rows = h.rearrange("g (s j) n -> (g s) j n", j=PACK)
         h_raw = [sb.tile([P, 2, N], F32, name="h_raw%d" % i) for i in range(2)]
         w_raw = {k: sb.tile([P, PACK, M], F32, name="w_raw_" + k) for k in "tc"}
-        x = [sb.tile([P, N], F32, name="x%d" % u) for u in range(PACK)]
-        bias = {k: sb.tile([P, PACK], F32, name="bias_" + k) for k in "tc"}
+        x = unit_tiles("x", units)
+        bias_low = {(k, g): sb.tile([P, 1], F32, name="bias_low_%s%d" % (k, g)) for k in "tc" for g in range(G)}
+        bias_high = {k: sb.tile([P, 2], F32, name="bias_high_" + k) for k in "tc"}
 
+        def load_biases(queue, k, b):
+            for g in range(G):
+                queue.dma_start(out=bias_low[k, g][:], in_=b[g].rearrange("(s u) o -> s u o", u=PACK)[:, 0:2, :])
+            queue.dma_start(out=bias_high[k][:], in_=b.rearrange("g (s u) o -> (g s) (u o)", u=PACK)[:, 2:4])
+
+        def low_rows(array, g):
+            return array.rearrange("(g s u) n -> g s u n", g=G, u=PACK)[g, :, 0:2, :]
+
+        def high_rows(array):
+            return array.rearrange("(p u) n -> p u n", u=PACK)[:, 2:4, :]
+
+        x_rows = xr.rearrange("g m n -> (g m) n")
         for i in range(2):
             nc.sync.dma_start(out=h_raw[i][:], in_=h_rows[:, 2 * i : 2 * i + 2, :])
-        for k, w, b in (("t", wt, bt), ("c", wc, bc)):
+        load_biases(nc.scalar, "t", bt)
+        for k, w in (("t", wt), ("c", wc)):
             nc.sync.dma_start(out=w_raw[k][:], in_=w.rearrange("g (s j) m -> (g s) j m", j=PACK))
-            nc.scalar.dma_start(out=bias[k][:], in_=b.rearrange("g (s u) o -> (g s) (u o)", u=PACK))
-        for u in range(PACK):
-            nc.sync.dma_start(out=x[u][:], in_=x_rows[:, u, :])
+        nc.sync.dma_start(out=x[LOW, 0][:], in_=low_rows(x_rows, 0))
+        load_biases(nc.sync, "c", bc)
+        nc.sync.dma_start(out=x[LOW, 1][:], in_=low_rows(x_rows, 1))
+        for u in (2, 3):
+            nc.sync.dma_start(out=x[HIGH, u][:], in_=high_rows(x_rows)[:, u - 2, :])
 
-        w_codes = {k: sb.tile([P, 6 * R], U32, name="w_codes_" + k, align_bytes=64) for k in "tc"}
-        w_scales = {k: sb.tile([P, 6 * R], U8, name="w_scales_" + k, align_bytes=64) for k in "tc"}
-        warm = sb.tile([P, 8], F32, name="warm")
-        warm_out = sb.tile([P, 8], F32, name="warm_out")
-        nc.vector.memset(warm[:], 0.0)
-        nc.scalar.activation(out=warm_out[:], in_=warm[:], func=ACT.Sigmoid)
-        for k in "tc":
-            nc.vector.memset(w_codes[k][:], 0)
-            nc.vector.memset(w_scales[k][:].bitcast(U32), 0)
+        def round_pair(copy, words, pair, rows):
+            copy(out=words[:, :, 2 * pair : 2 * pair + 2], in_=rows.rearrange("p j n -> p n j"))
 
-        h_bf = sb.tile([P, N, PACK], BF16, name="h_bf", align_bytes=64)
+        h_bf = [sb.tile([P, HALF, PACK], BF16, name="h_bf%d" % i, align_bytes=64) for i in range(2)]
         h_codes = sb.tile([P, N], U32, name="h_codes", align_bytes=64)
         h_scales = sb.tile([P, N], U8, name="h_scales", align_bytes=64)
-        nc.vector.tensor_copy(out=h_bf[:, :, 0:2], in_=h_raw[0][:].rearrange("p j n -> p n j"))
-        nc.vector.tensor_copy(out=h_bf[:, :H_SPLIT, 2:4], in_=h_raw[1][:, :, :H_SPLIT].rearrange("p j n -> p n j"))
-        nc.scalar.copy(out=h_bf[:, H_SPLIT:, 2:4], in_=h_raw[1][:, :, H_SPLIT:].rearrange("p j n -> p n j"))
-        nc.vector.quantize_mx(out=h_codes[:].bitcast(FP8X4), scales=h_scales[:], in_=h_bf[:].rearrange("p n j -> p (n j)"))
-
-        def quantise_weights(k):
-            w_bf = sb.tile([P, PACK, R, PACK], BF16, name="w_bf_" + k, align_bytes=64)
-            dst = w_bf[:].rearrange("p u s j -> p s j u")
-            src = w_raw[k][:].rearrange("p j (s u) -> p s j u", u=PACK)
-            nc.vector.tensor_copy(out=dst[:, :W_SPLIT], in_=src[:, :W_SPLIT])
-            nc.scalar.copy(out=dst[:, W_SPLIT:], in_=src[:, W_SPLIT:])
+        for i in range(2):
+            round_pair(nc.vector.tensor_copy, h_bf[i], 0, h_raw[0][:, :, halves[i]])
+        round_pair(nc.scalar.copy, h_bf[1][:, H_SPLIT - HALF :], 1, h_raw[1][:, :, H_SPLIT:])
+        round_pair(nc.vector.tensor_copy, h_bf[0], 1, h_raw[1][:, :, :HALF])
+        round_pair(nc.vector.tensor_copy, h_bf[1][:, : H_SPLIT - HALF], 1, h_raw[1][:, :, HALF:H_SPLIT])
+        for i in range(2):
             nc.vector.quantize_mx(
-                out=w_codes[k][:, R : 5 * R].bitcast(FP8X4),
-                scales=w_scales[k][:, R : 5 * R],
-                in_=w_bf[:].rearrange("p u s j -> p (u s j)"),
+                out=h_codes[:, halves[i]].bitcast(FP8X4),
+                scales=h_scales[:, halves[i]],
+                in_=h_bf[i][:].rearrange("p n j -> p (n j)"),
             )
+
+        w_codes = sb.tile([P, 2 * M], U32, name="w_codes", align_bytes=64)
+        w_scales = sb.tile([P, 2 * M], U8, name="w_scales", align_bytes=64)
+        w_start = {("t", LOW): 0, ("t", HIGH): P, ("c", HIGH): 2 * P, ("c", LOW): 3 * P}
+        w_bf = {key: sb.tile([P, P * PACK], BF16, name="w_bf_%s%d" % key, align_bytes=64) for key in w_start}
+
+        def round_weights(k):
+            src = w_raw[k][:].rearrange("p j (s u) -> p s u j", u=PACK)
+            low = w_bf[k, LOW][:].rearrange("p (s u j) -> p s u j", u=2, j=PACK)
+            high = w_bf[k, HIGH][:].rearrange("p (u s j) -> p s u j", u=2, j=PACK)
+            nc.vector.tensor_copy(out=low, in_=src[:, :, 0:2, :])
+            nc.vector.tensor_copy(out=high, in_=src[:, :, 2:4, :])
+
+        def quantise_weights(k, which):
+            window = slice(w_start[k, which], w_start[k, which] + P)
+            nc.vector.quantize_mx(out=w_codes[:, window].bitcast(FP8X4), scales=w_scales[:, window], in_=w_bf[k, which][:])
 
         z = {}
 
-        def product(k, u):
+        def product(k, which, u=None):
             for g in range(G):
-                rows = slice(R * g, R * g + R)
-                cols = slice(R * (u + 1 - g), R * (u + 3 - g))
+                first = w_start[k, which] + (0 if which == LOW else R * (u - 2 - g))
+                cols = slice(first, first + P)
                 z[k, u, g] = ps.tile([P, N], F32, name="z_%s%d" % (k, g))
                 nc.tensor.matmul_mx(
                     out=z[k, u, g][:],
-                    lhsT=w_codes[k][rows, cols].bitcast(FP8X4),
-                    lhsT_scale=w_scales[k][rows, cols],
-                    rhs=h_codes[rows, :].bitcast(FP8X4),
-                    rhs_scale=h_scales[rows, :],
+                    lhsT=w_codes[rows_of[g], cols].bitcast(FP8X4),
+                    lhsT_scale=w_scales[rows_of[g], cols],
+                    rhs=h_codes[rows_of[g], :].bitcast(FP8X4),
+                    rhs_scale=h_scales[rows_of[g], :],
                     start=True,
                     stop=True,
                 )
 
-        t = [sb.tile([P, N], F32, name="t%d" % u) for u in range(PACK)]
-        r = [sb.tile([P, N], F32, name="r%d" % u) for u in range(2)]
-        a = [sb.tile([P, N], F32, name="a%d" % u) for u in range(PACK)]
-        b = [sb.tile([P, N], F32, name="b%d" % u) for u in range(PACK)]
-        y_lo = sb.tile([P, 2, N], F32, name="y_lo")
-        y_hi = [sb.tile([P, 2, HALF], F32, name="y_hi%d" % i) for i in range(2)]
+        gate = unit_tiles("gate", units)
+        relu = unit_tiles("relu", units[2:])
+        gated = unit_tiles("gated", units)
+        carried = unit_tiles("carried", units)
+        y_low = [sb.tile([P, N], F32, name="y_low%d" % g) for g in range(G)]
+        y_moved = sb.tile([P, 2, N], F32, name="y_moved")
+        y_high = [sb.tile([P, 2, HALF], F32, name="y_high%d" % i) for i in range(2)]
         y_bf = [sb.tile([P, HALF, PACK], BF16, name="y_bf%d" % i, align_bytes=64) for i in range(2)]
         y_codes = sb.tile([P, N], U32, name="y_codes", align_bytes=64)
         y_scales = sb.tile([P, N], U8, name="y_scales", align_bytes=64)
 
-        def from_psum(func, k, u, dst):
-            for g in range(G):
-                rows = slice(R * g, R * g + R)
-                nc.scalar.activation(out=dst[rows, :], in_=z[k, u, g][rows, :], func=func, bias=bias[k][rows, u : u + 1])
+        def sums(k, unit):
+            which, index = unit
+            if which == LOW:
+                return [(slice(0, P), z[k, None, index], bias_low[k, index][:])]
+            return [(rows_of[g], z[k, index, g], bias_high[k][rows_of[g], index - 2 : index - 1]) for g in range(G)]
 
-        def gated_from_psum(u):
-            for g in range(G):
-                rows = slice(R * g, R * g + R)
+        def activate(func, k, dst, unit, cols=whole):
+            for rows, bank, bias in sums(k, unit):
+                nc.scalar.activation(out=dst[unit][rows, cols], in_=bank[rows, cols], func=func, bias=bias)
+
+        def gate_sums(unit, cols=whole):
+            for rows, bank, bias in sums("c", unit):
                 nc.vector.scalar_tensor_tensor(
-                    out=a[u][rows, :], in0=z["c", u, g][rows, :], scalar=bias["c"][rows, u : u + 1], in1=t[u][rows, :],
+                    out=gated[unit][rows, cols], in0=bank[rows, cols], scalar=bias, in1=gate[unit][rows, cols],
                     op0=ALU.add, op1=ALU.mult,
                 )
 
-        def carried(u, cols):
+        def gate_relu(unit, cols):
+            nc.vector.tensor_tensor(out=gated[unit][:, cols], in0=relu[unit][:, cols], in1=gate[unit][:, cols], op=ALU.mult)
+
+        def carry(unit, cols=whole):
             nc.vector.scalar_tensor_tensor(
-                out=b[u][:, cols], in0=t[u][:, cols], scalar=1.0, in1=x[u][:, cols], op0=ALU.subtract, op1=ALU.mult
+                out=carried[unit][:, cols], in0=gate[unit][:, cols], scalar=1.0, in1=x[unit][:, cols],
+                op0=ALU.subtract, op1=ALU.mult,
             )
 
-        def gated(u, cols):
-            nc.vector.tensor_tensor(out=a[u][:, cols], in0=r[u - 2][:, cols], in1=t[u][:, cols], op=ALU.mult)
-
-        def combine(u, cols, dst):
+        def combine(dst, unit, cols):
             nc.vector.scalar_tensor_tensor(
-                out=dst, in0=a[u][:, cols], scalar=0.0, in1=b[u][:, cols], op0=ALU.max, op1=ALU.subtract
+                out=dst, in0=gated[unit][:, cols], scalar=0.0, in1=carried[unit][:, cols], op0=ALU.max, op1=ALU.subtract
             )
 
-        whole = slice(0, N)
-        halves = [slice(0, HALF), slice(HALF, N)]
+        def combine_low(g):
+            combine(y_low[g][:], (LOW, g), whole)
+            nc.sync.dma_start(out=y_moved[rows_of[g]].bitcast(I32), in_=y_low[g][:].bitcast(I32))
 
-        quantise_weights("t")
-        product("t", 0)
-        product("t", 1)
-        quantise_weights("c")
-        from_psum(ACT.Sigmoid, "t", 0, t[0])
-        product("c", 0)
-        product("c", 1)
-        from_psum(ACT.Sigmoid, "t", 1, t[1])
-        product("t", 2)
-        product("t", 3)
-        from_psum(ACT.Sigmoid, "t", 2, t[2])
-        from_psum(ACT.Sigmoid, "t", 3, t[3])
-        for u in range(2):
-            gated_from_psum(u)
-            carried(u, whole)
-            product("c", u + 2)
-            if u == 1:
-                combine(0, whole, y_lo[:, 0, :])
-                nc.sync.dma_start(out=y_rows[:, 0, :], in_=y_lo[:, 0, :])
-        carried(2, whole)
-        combine(1, whole, y_lo[:, 1, :])
-        nc.sync.dma_start(out=y_rows[:, 1, :], in_=y_lo[:, 1, :])
-        from_psum(ACT.Relu, "c", 2, r[0])
-        from_psum(ACT.Relu, "c", 3, r[1])
-        carried(3, whole)
-        for i in range(2):
-            nc.scalar.copy(out=y_bf[i][:, :, 0:2], in_=y_lo[:, :, halves[i]].rearrange("p u n -> p n u"))
-        for i in range(2):
-            gated(2, halves[i])
-            gated(3, halves[i])
-            combine(2, halves[i], y_hi[i][:, 0, :])
-            combine(3, halves[i], y_hi[i][:, 1, :])
-            nc.sync.dma_start(out=y_rows[:, 2:4, halves[i]], in_=y_hi[i][:])
-            cast = nc.scalar.copy if i == 0 else nc.vector.tensor_copy
-            cast(out=y_bf[i][:, :, 2:4], in_=y_hi[i][:].rearrange("p u n -> p n u"))
+        def combine_high(i, order):
+            for u in order:
+                combine(y_high[i][:, u - 2, :], (HIGH, u), halves[i])
+            nc.sync.dma_start(out=high_rows(out_0)[:, :, halves[i]], in_=y_high[i][:])
+
+        round_weights("t")
+        quantise_weights("t", LOW)
+        product("t", LOW)
+        quantise_weights("t", HIGH)
+        product("t", HIGH, 2)
+        round_weights("c")
+        quantise_weights("c", LOW)
+        product("c", LOW)
+        for half in halves:
+            activate(ACT.Sigmoid, "t", gate, (LOW, 0), half)
+        activate(ACT.Sigmoid, "t", gate, (LOW, 1))
+        quantise_weights("c", HIGH)
+        product("t", HIGH, 3)
+        product("c", HIGH, 2)
+        for u in (2, 3):
+            activate(ACT.Sigmoid, "t", gate, (HIGH, u))
+        activate(ACT.Relu, "c", relu, (HIGH, 2))
+
+        for half in halves:
+            carry((LOW, 0), half)
+        gate_sums((LOW, 0))
+        carry((LOW, 1))
+        combine_low(0)
+        gate_sums((LOW, 1))
+        product("c", HIGH, 3)
+        carry((HIGH, 2))
+        combine_low(1)
+        for g in range(G):
+            nc.sync.dma_start(out=low_rows(out_0, g), in_=y_low[g][:])
+
+        carry((HIGH, 3))
+        gate_sums((HIGH, 3), halves[0])
+        activate(ACT.Relu, "c", relu, (HIGH, 3), halves[1])
+        gate_relu((HIGH, 2), halves[0])
+        combine_high(0, (3, 2))
+        round_pair(nc.scalar.copy, y_bf[0], HIGH, y_high[0][:])
+        round_pair(nc.scalar.copy, y_bf[0], LOW, y_moved[:, :, halves[0]])
+        for u in (2, 3):
+            gate_relu((HIGH, u), halves[1])
+        combine_high(1, (2, 3))
+        round_pair(nc.vector.tensor_copy, y_bf[1], LOW, y_moved[:, :, halves[1]])
+        round_pair(nc.vector.tensor_copy, y_bf[1], HIGH, y_high[1][:])
+
         words = out_1.rearrange("o p n u -> (o p) (n u)").bitcast(I32)
         for i in range(2):
             nc.vector.quantize_mx(
-                out=y_codes[:, halves[i]].bitcast(FP8X4), scales=y_scales[:, halves[i]],
+                out=y_codes[:, halves[i]].bitcast(FP8X4),
+                scales=y_scales[:, halves[i]],
                 in_=y_bf[i][:].rearrange("p n u -> p (n u)"),
             )
             nc.sync.dma_start(out=words[:, halves[i]], in_=y_codes[:, halves[i]].bitcast(I32))

from contextlib import ExitStack

import concourse.mybir as mybir

G, D, M, N = 2, 256, 256, 512
FLOPS = 2 * 2 * G * D * M * N

F32 = mybir.dt.float32
BF16 = mybir.dt.bfloat16
U32 = mybir.dt.uint32
I32 = mybir.dt.int32
U8 = mybir.dt.uint8
FP8X4 = mybir.dt.float8_e4m3fn_x4
ACT = mybir.ActivationFunctionType
ALU = mybir.AluOpType

P = 128
R = 64
PACK = 4
HALF = N // 2
H_SPLIT = 352
LOW, HIGH = 0, 1


def tile_rows_pl_cell_hwy_kernel(tc, h, wt, wc, xr, bt, bc, out_0, out_1, out_2):
    nc = tc.nc
    with ExitStack() as ctx:
        sb = ctx.enter_context(tc.tile_pool(name="sb", bufs=1))
        ps = ctx.enter_context(tc.psum_pool(name="ps", bufs=2))
        ctx.enter_context(tc.manual_schedule())

        whole = slice(0, N)
        halves = [slice(0, HALF), slice(HALF, N)]
        rows_of = [slice(R * g, R * (g + 1)) for g in range(G)]

        units = [(LOW, 0), (LOW, 1), (HIGH, 2), (HIGH, 3)]

        def unit_tiles(name, which):
            return {unit: sb.tile([P, N], F32, name="%s%d" % (name, unit[1])) for unit in which}

        h_rows = h.rearrange("g (s j) n -> (g s) j n", j=PACK)
        h_raw = [sb.tile([P, 2, N], F32, name="h_raw%d" % i) for i in range(2)]
        w_raw = {k: sb.tile([P, PACK, M], F32, name="w_raw_" + k) for k in "tc"}
        x = unit_tiles("x", units)
        bias_low = {(k, g): sb.tile([P, 1], F32, name="bias_low_%s%d" % (k, g)) for k in "tc" for g in range(G)}
        bias_high = {k: sb.tile([P, 2], F32, name="bias_high_" + k) for k in "tc"}

        def load_biases(queue, k, b):
            for g in range(G):
                queue.dma_start(out=bias_low[k, g][:], in_=b[g].rearrange("(s u) o -> s u o", u=PACK)[:, 0:2, :])
            queue.dma_start(out=bias_high[k][:], in_=b.rearrange("g (s u) o -> (g s) (u o)", u=PACK)[:, 2:4])

        def low_rows(array, g):
            return array.rearrange("(g s u) n -> g s u n", g=G, u=PACK)[g, :, 0:2, :]

        def high_rows(array):
            return array.rearrange("(p u) n -> p u n", u=PACK)[:, 2:4, :]

        x_rows = xr.rearrange("g m n -> (g m) n")
        for i in range(2):
            nc.sync.dma_start(out=h_raw[i][:], in_=h_rows[:, 2 * i : 2 * i + 2, :])
        load_biases(nc.scalar, "t", bt)
        for k, w in (("t", wt), ("c", wc)):
            nc.sync.dma_start(out=w_raw[k][:], in_=w.rearrange("g (s j) m -> (g s) j m", j=PACK))
        nc.sync.dma_start(out=x[LOW, 0][:], in_=low_rows(x_rows, 0))
        load_biases(nc.sync, "c", bc)
        nc.sync.dma_start(out=x[LOW, 1][:], in_=low_rows(x_rows, 1))
        for u in (2, 3):
            nc.sync.dma_start(out=x[HIGH, u][:], in_=high_rows(x_rows)[:, u - 2, :])

        def round_pair(copy, words, pair, rows):
            copy(out=words[:, :, 2 * pair : 2 * pair + 2], in_=rows.rearrange("p j n -> p n j"))

        h_bf = [sb.tile([P, HALF, PACK], BF16, name="h_bf%d" % i, align_bytes=64) for i in range(2)]
        h_codes = sb.tile([P, N], U32, name="h_codes", align_bytes=64)
        h_scales = sb.tile([P, N], U8, name="h_scales", align_bytes=64)
        for i in range(2):
            round_pair(nc.vector.tensor_copy, h_bf[i], 0, h_raw[0][:, :, halves[i]])
        round_pair(nc.scalar.copy, h_bf[1][:, H_SPLIT - HALF :], 1, h_raw[1][:, :, H_SPLIT:])
        round_pair(nc.vector.tensor_copy, h_bf[0], 1, h_raw[1][:, :, :HALF])
        round_pair(nc.vector.tensor_copy, h_bf[1][:, : H_SPLIT - HALF], 1, h_raw[1][:, :, HALF:H_SPLIT])
        for i in range(2):
            nc.vector.quantize_mx(
                out=h_codes[:, halves[i]].bitcast(FP8X4),
                scales=h_scales[:, halves[i]],
                in_=h_bf[i][:].rearrange("p n j -> p (n j)"),
            )

        w_codes = sb.tile([P, 2 * M], U32, name="w_codes", align_bytes=64)
        w_scales = sb.tile([P, 2 * M], U8, name="w_scales", align_bytes=64)
        w_start = {("t", LOW): 0, ("t", HIGH): P, ("c", HIGH): 2 * P, ("c", LOW): 3 * P}
        w_bf = {key: sb.tile([P, P * PACK], BF16, name="w_bf_%s%d" % key, align_bytes=64) for key in w_start}

        def round_weights(k):
            src = w_raw[k][:].rearrange("p j (s u) -> p s u j", u=PACK)
            low = w_bf[k, LOW][:].rearrange("p (s u j) -> p s u j", u=2, j=PACK)
            high = w_bf[k, HIGH][:].rearrange("p (u s j) -> p s u j", u=2, j=PACK)
            nc.vector.tensor_copy(out=low, in_=src[:, :, 0:2, :])
            nc.vector.tensor_copy(out=high, in_=src[:, :, 2:4, :])

        def quantise_weights(k, which):
            window = slice(w_start[k, which], w_start[k, which] + P)
            nc.vector.quantize_mx(out=w_codes[:, window].bitcast(FP8X4), scales=w_scales[:, window], in_=w_bf[k, which][:])

        z = {}

        def product(k, which, u=None):
            for g in range(G):
                first = w_start[k, which] + (0 if which == LOW else R * (u - 2 - g))
                cols = slice(first, first + P)
                z[k, u, g] = ps.tile([P, N], F32, name="z_%s%d" % (k, g))
                nc.tensor.matmul_mx(
                    out=z[k, u, g][:],
                    lhsT=w_codes[rows_of[g], cols].bitcast(FP8X4),
                    lhsT_scale=w_scales[rows_of[g], cols],
                    rhs=h_codes[rows_of[g], :].bitcast(FP8X4),
                    rhs_scale=h_scales[rows_of[g], :],
                    start=True,
                    stop=True,
                )

        gate = unit_tiles("gate", units)
        relu = unit_tiles("relu", units[2:])
        gated = unit_tiles("gated", units)
        carried = unit_tiles("carried", units)
        y_low = [sb.tile([P, N], F32, name="y_low%d" % g) for g in range(G)]
        y_moved = sb.tile([P, 2, N], F32, name="y_moved")
        y_high = [sb.tile([P, 2, HALF], F32, name="y_high%d" % i) for i in range(2)]
        y_bf = [sb.tile([P, HALF, PACK], BF16, name="y_bf%d" % i, align_bytes=64) for i in range(2)]
        y_codes = sb.tile([P, N], U32, name="y_codes", align_bytes=64)
        y_scales = sb.tile([P, N], U8, name="y_scales", align_bytes=64)

        def sums(k, unit):
            which, index = unit
            if which == LOW:
                return [(slice(0, P), z[k, None, index], bias_low[k, index][:])]
            return [(rows_of[g], z[k, index, g], bias_high[k][rows_of[g], index - 2 : index - 1]) for g in range(G)]

        def activate(func, k, dst, unit, cols=whole):
            for rows, bank, bias in sums(k, unit):
                nc.scalar.activation(out=dst[unit][rows, cols], in_=bank[rows, cols], func=func, bias=bias)

        def gate_sums(unit, cols=whole):
            for rows, bank, bias in sums("c", unit):
                nc.vector.scalar_tensor_tensor(
                    out=gated[unit][rows, cols], in0=bank[rows, cols], scalar=bias, in1=gate[unit][rows, cols],
                    op0=ALU.add, op1=ALU.mult,
                )

        def gate_relu(unit, cols):
            nc.vector.tensor_tensor(out=gated[unit][:, cols], in0=relu[unit][:, cols], in1=gate[unit][:, cols], op=ALU.mult)

        def carry(unit, cols=whole):
            nc.vector.scalar_tensor_tensor(
                out=carried[unit][:, cols], in0=gate[unit][:, cols], scalar=1.0, in1=x[unit][:, cols],
                op0=ALU.subtract, op1=ALU.mult,
            )

        def combine(dst, unit, cols):
            nc.vector.scalar_tensor_tensor(
                out=dst, in0=gated[unit][:, cols], scalar=0.0, in1=carried[unit][:, cols], op0=ALU.max, op1=ALU.subtract
            )

        def combine_low(g):
            combine(y_low[g][:], (LOW, g), whole)
            nc.sync.dma_start(out=y_moved[rows_of[g]].bitcast(I32), in_=y_low[g][:].bitcast(I32))

        def combine_high(i, order):
            for u in order:
                combine(y_high[i][:, u - 2, :], (HIGH, u), halves[i])
            nc.sync.dma_start(out=high_rows(out_0)[:, :, halves[i]], in_=y_high[i][:])

        round_weights("t")
        quantise_weights("t", LOW)
        product("t", LOW)
        quantise_weights("t", HIGH)
        product("t", HIGH, 2)
        round_weights("c")
        quantise_weights("c", LOW)
        product("c", LOW)
        for half in halves:
            activate(ACT.Sigmoid, "t", gate, (LOW, 0), half)
        activate(ACT.Sigmoid, "t", gate, (LOW, 1))
        quantise_weights("c", HIGH)
        product("t", HIGH, 3)
        product("c", HIGH, 2)
        for u in (2, 3):
            activate(ACT.Sigmoid, "t", gate, (HIGH, u))
        activate(ACT.Relu, "c", relu, (HIGH, 2))

        for half in halves:
            carry((LOW, 0), half)
        gate_sums((LOW, 0))
        carry((LOW, 1))
        combine_low(0)
        gate_sums((LOW, 1))
        product("c", HIGH, 3)
        carry((HIGH, 2))
        combine_low(1)
        for g in range(G):
            nc.sync.dma_start(out=low_rows(out_0, g), in_=y_low[g][:])

        carry((HIGH, 3))
        gate_sums((HIGH, 3), halves[0])
        activate(ACT.Relu, "c", relu, (HIGH, 3), halves[1])
        gate_relu((HIGH, 2), halves[0])
        combine_high(0, (3, 2))
        round_pair(nc.scalar.copy, y_bf[0], HIGH, y_high[0][:])
        round_pair(nc.scalar.copy, y_bf[0], LOW, y_moved[:, :, halves[0]])
        for u in (2, 3):
            gate_relu((HIGH, u), halves[1])
        combine_high(1, (2, 3))
        round_pair(nc.vector.tensor_copy, y_bf[1], LOW, y_moved[:, :, halves[1]])
        round_pair(nc.vector.tensor_copy, y_bf[1], HIGH, y_high[1][:])

        words = out_1.rearrange("o p n u -> (o p) (n u)").bitcast(I32)
        for i in range(2):
            nc.vector.quantize_mx(
                out=y_codes[:, halves[i]].bitcast(FP8X4),
                scales=y_scales[:, halves[i]],
                in_=y_bf[i][:].rearrange("p n u -> p (n u)"),
            )
            nc.sync.dma_start(out=words[:, halves[i]], in_=y_codes[:, halves[i]].bitcast(I32))
        scale_rows = out_2.rearrange("o f n -> (o f) n").bitcast(I32)
        for q in range(4):
            queue = nc.scalar if q % 2 else nc.sync
            queue.dma_start(out=scale_rows[4 * q : 4 * q + 4, :], in_=y_scales[32 * q : 32 * q + 4, :].bitcast(I32))
